import numpy as np
import ml_dtypes


def mxq(x, axis, fmt="e4m3"):
    dtype, down = {"e4m3": (ml_dtypes.float8_e4m3fn, 7), "e5m2": (ml_dtypes.float8_e5m2, 14)}[fmt]
    v = np.moveaxis(np.asarray(x, np.float32).astype(ml_dtypes.bfloat16).astype(np.float64), axis, -1)
    blocks = v.reshape(v.shape[:-1] + (-1, 32))
    amax = np.abs(blocks).max(-1, keepdims=True)
    byte = np.maximum(np.where(amax > 0, np.frexp(amax)[1] - 1 + 127, 0) - down, 1)
    scale = np.exp2(byte - 127.0)
    codes = (blocks / scale).astype(np.float32).astype(dtype).astype(np.float64)
    return np.moveaxis((codes * scale).reshape(v.shape), -1, axis)


WIDE = False


def mx_kscale(k):
    if not WIDE:
        return np.ones(k)
    levels = np.array([10, -10, 5, -5, 0])
    if k % 512:
        return np.exp2(np.random.permutation(np.resize(levels, k // 32))).repeat(32)
    a = np.empty((k // 512, 16))
    for p in range(k // 512):
        a[p, :8] = np.random.permutation(np.resize(levels, 8))
        for g in range(8):
            far = levels[np.abs(levels - a[p, g]) >= 10]
            a[p, g + 8] = far[np.random.randint(len(far))]
    return np.exp2(a.ravel()).repeat(32)


def f64(x):
    return np.asarray(x).astype(np.float64)


def striped(idx):
    return np.tile(idx.reshape(-1, 16).T, (8, 1)).astype(np.uint16)


def unstriped(offs):
    return offs[:16].T.reshape(-1).astype(np.int64)


E2M1 = np.array([0.0, 0.5, 1.0, 1.5, 2.0, 3.0, 4.0, 6.0, -0.0, -0.5, -1.0, -1.5, -2.0, -3.0, -4.0, -6.0])


def pack_weight(w, fmt):
    k, n = w.shape
    w = f64(np.asarray(w, np.float32).astype(ml_dtypes.bfloat16)).reshape(k // 32, 32, n)
    amax = np.abs(w).max(1)
    if fmt == "e4m3":
        byte = np.frexp(amax)[1] - 1 + 127 - 7
    else:
        mant, ex = np.frexp(amax / 6.0)
        byte = np.where(mant > 0.5, ex, ex - 1) + 127
    byte = np.clip(np.where(amax > 0, byte, 1), 1, 254)
    scaled = (w * np.exp2(127.0 - byte)[:, None, :]).reshape(k, n).astype(np.float32)
    by_word = np.ascontiguousarray(scaled.reshape(k // 512, 128, 4, n).transpose(0, 1, 3, 2))
    if fmt == "e4m3":
        words = by_word.astype(ml_dtypes.float8_e4m3fn).view(np.uint8)
    else:
        c = by_word.astype(ml_dtypes.float4_e2m1fn).view(np.uint8) & 0xF
        words = (c[..., 0::2] | (c[..., 1::2] << 4)).reshape(k // 512, 128, 2 * n)
    return np.ascontiguousarray(words), np.ascontiguousarray(byte.astype(np.uint8).reshape(k // 512, 16, n))


def unpack_weight(words, scales, fmt):
    g, _, n = scales.shape
    words = np.ascontiguousarray(words).reshape(g, 128, n, -1)
    if fmt == "e4m3":
        vals = words.view(ml_dtypes.float8_e4m3fn).astype(np.float64)
    else:
        nib = np.empty((g, 128, n, 4), np.uint8)
        nib[..., 0::2] = words & 0xF
        nib[..., 1::2] = words >> 4
        vals = E2M1[nib]
    vals = vals * np.repeat(np.exp2(scales.astype(np.float64) - 127.0), 8, axis=1)[..., None]
    return vals.transpose(0, 1, 3, 2).reshape(g * 512, n)


def gelu(v):
    return 0.5 * v * (1.0 + np.tanh(np.sqrt(2.0 / np.pi) * (v + 0.044715 * v**3)))


def striped8(idx):
    return np.concatenate([v.reshape(-1, 16).T for v in idx]).astype(np.uint16)


def unstriped8(offs):
    return np.stack([offs[16 * g:16 * g + 16].T.reshape(-1) for g in range(8)]).astype(np.int64)


def runs(v, idx8):
    k = np.arange(v.shape[0])
    return v[k[:, None], idx8[k % 512 // 64]]


T, S, P, K, H, N = 2048, 1024, 512, 512, 1024, 768


def setup_inputs():
    n = np.random.standard_normal
    s = mx_kscale(K)[:, None]
    u = mx_kscale(H)[:, None]
    d = {}
    d["tab_words"], d["tab_scales"] = pack_weight(n((K, T)) * s, "e4m3")
    d["offs"] = striped8(np.stack([np.random.permutation(T)[:S] for _ in range(8)]))
    d["pos1"] = striped(np.random.permutation(S)[:P])
    d["pos2"] = striped(np.random.permutation(S)[:P])
    d["w1"] = (1.4 * n((K, H)) / K**0.5 / s).astype(np.float32)
    d["swing"] = (np.exp(0.4 * n(H)) * u[:, 0]).astype(np.float32)
    d["w2_words"], d["w2_scales"] = pack_weight(1.3 * n((H, H)) / H**0.5 / u, "e2m1")
    d["panel"] = (np.exp(0.4 * n(H)) * u[:, 0]).astype(np.float32)
    d["w3"] = (0.7 * n((H, N)) / H**0.5 / u).astype(np.float32)
    d["base"] = n((N, P)).astype(np.float32)
    return d


def reference(tab_words, tab_scales, offs, pos1, pos2, w1, swing, w2_words, w2_scales, panel, w3, base):
    v = runs(unpack_weight(tab_words, tab_scales, "e4m3"), unstriped8(offs))
    a = mxq(f64(w1), 0, "e4m3").T @ v
    f = a / (1.0 + np.exp(-a)) * f64(swing)[:, None]
    w2 = unpack_weight(w2_words, w2_scales, "e2m1")
    b = w2.T @ mxq(f, 0, "e4m3")
    h = np.maximum(a, b) * f64(panel)[:, None]
    z = h[:, unstriped(pos1)] + h[:, unstriped(pos2)]
    y = mxq(f64(w3), 0, "e4m3").T @ mxq(z, 0, "e4m3")
    return y - f64(base)

@@ -1,0 +1,304 @@
+from contextlib import ExitStack
+
+import concourse.mybir as mybir
+
+T, S, PAIRS, K, H, N = 2048, 1024, 512, 512, 1024, 768
+FLOPS = 2 * (K * H * S + H * H * S + H * N * PAIRS)
+
+F32 = mybir.dt.float32
+BF16 = mybir.dt.bfloat16
+I32 = mybir.dt.int32
+U32 = mybir.dt.uint32
+U16 = mybir.dt.uint16
+U8 = mybir.dt.uint8
+FP8X4 = mybir.dt.float8_e4m3fn_x4
+FP4X4 = mybir.dt.float4_e2m1fn_x4
+ACT = mybir.ActivationFunctionType
+ALU = mybir.AluOpType
+
+P = 128
+PACK = 4
+KP = P * PACK
+G = H // KP
+HALF = 512
+BLK = 128
+STEP = 256
+PAIR_CHUNKS = ((0, 256), (256, 128), (384, 128))
+NT = N // P
+
+
+def tile_list_mirrored_figure_deviations_kernel(
+    tc, tab_words, tab_scales, offs, pos1, pos2, w1, swing, w2_words, w2_scales, panel, w3, base, out
+):
+    nc = tc.nc
+    with ExitStack() as ctx:
+        keep = ctx.enter_context(tc.tile_pool(name="keep", bufs=1))
+        ring = ctx.enter_context(tc.tile_pool(name="ring", bufs=2))
+        ring3 = ctx.enter_context(tc.tile_pool(name="ring3", bufs=3))
+        psum = ctx.enter_context(tc.psum_pool(name="psum", bufs=4))
+
+        offs_sb = keep.tile([P, S // 16], U16, name="offs_sb")
+        pos1_sb = keep.tile([P, PAIRS // 16], U16, name="pos1_sb")
+        pos2_sb = keep.tile([P, PAIRS // 16], U16, name="pos2_sb")
+        swing_sb = keep.tile([P, G, PACK], F32, name="swing_sb")
+        panel_sb = keep.tile([P, G, PACK], F32, name="panel_sb")
+        tab_sc = keep.tile([P, T], U8, name="tab_sc", tag="scale_rows")
+        tab_w = keep.tile([P, T], U32, name="tab_w")
+
+        nc.vector.memset(tab_sc[:].bitcast(I32), 0)
+        nc.sync.dma_start(offs_sb[:], offs)
+        sc_rows = tab_scales[0].rearrange("(g r) t -> r g t", r=2)
+        for r in range(2):
+            nc.scalar.dma_start(tab_sc[r:P:16, :].bitcast(I32), sc_rows[r].bitcast(I32))
+        nc.gpsimd.dma_start(swing_sb[:], swing.rearrange("(g p t) -> p g t", p=P, t=PACK))
+        nc.gpsimd.dma_start(panel_sb[:], panel.rearrange("(g p t) -> p g t", p=P, t=PACK))
+        nc.sync.dma_start(pos1_sb[:], pos1)
+        nc.sync.dma_start(pos2_sb[:], pos2)
+
+        w1_raw = [ring.tile([P, PACK, KP], F32, name=f"w1_raw{g}", tag="raw") for g in range(G)]
+        w1_rows = w1.rearrange("(p j) c -> p j c", j=PACK)
+        nc.sync.dma_start(tab_w[:].bitcast(I32), tab_words[0].rearrange("p n t -> p (n t)").bitcast(I32))
+        nc.sync.dma_start(w1_raw[0][:], w1_rows[:, :, 0:KP])
+        nc.sync.dma_start(w1_raw[1][:], w1_rows[:, :, KP : 2 * KP])
+
+        v_sc = []
+        for c in range(2):
+            picked = keep.tile([P, HALF], U8, name=f"picked_sc{c}")
+            nc.vector.tensor_copy(picked[:], tab_sc[:].indirect(offs_sb[:, 32 * c : 32 * (c + 1)]))
+            plane = keep.tile([P, HALF], U8, name=f"v_sc{c}", align_bytes=64)
+            nc.vector.tensor_copy(plane[:].bitcast(I32), picked[:].bitcast(I32))
+            for r in range(2):
+                nc.scalar.dma_start(plane[2 + r : P : 32, :].bitcast(I32), picked[16 + r : P : 32, :].bitcast(I32))
+            v_sc.append(plane)
+
+        w2_raw = ring.tile([P, G, 2 * H], U8, name="w2_raw", tag="raw")
+        nc.sync.dma_start(w2_raw[:].bitcast(I32), w2_words.rearrange("a p c -> p a c").bitcast(I32))
+        w2_sc_raw = keep.tile([P, G, H], U8, name="w2_sc_raw", tag="scale_rows")
+        nc.vector.memset(w2_sc_raw[:].bitcast(I32), 0)
+        w2_sc_rows = w2_scales.rearrange("a (q r) c -> r q a c", r=4)
+        for r in range(4):
+            nc.sync.dma_start(w2_sc_raw[r:P:32, :, :].bitcast(I32), w2_sc_rows[r].bitcast(I32))
+
+        def w1_operand(g):
+            grouped = ring.tile([P, KP * PACK], BF16, name=f"w1_bf{g}", tag="w1_bf", align_bytes=64)
+            dst = grouped[:].rearrange("p (t m j) -> p m j t", t=PACK, j=PACK)
+            src = w1_raw[g][:].rearrange("p j (m t) -> p m j t", t=PACK)
+            if g == 0:
+                nc.scalar.copy(out=dst[:, 0:64], in_=src[:, 0:64])
+                nc.vector.tensor_copy(out=dst[:, 64:128], in_=src[:, 64:128])
+            else:
+                nc.vector.tensor_copy(out=dst, in_=src)
+            codes = keep.tile([P, KP], U32, name=f"w1_codes{g}", align_bytes=64)
+            scales = keep.tile([P, KP], U8, name=f"w1_sc{g}", align_bytes=64)
+            nc.vector.quantize_mx(out=codes[:].bitcast(FP8X4), scales=scales[:], in_=grouped[:])
+            return codes, scales
+
+        def pick_words(c):
+            words = keep.tile([P, HALF], U32, name=f"v_words{c}", align_bytes=64)
+            nc.vector.tensor_copy(words[:], tab_w[:].indirect(offs_sb[:, 32 * c : 32 * (c + 1)]))
+            return words
+
+        v_w = [pick_words(0), pick_words(1)]
+        w1_q = [w1_operand(0)]
+
+        a_sb = {}
+        f_bf = {}
+        f_codes = {}
+        f_sc = {}
+        for c in range(2):
+            for g in range(G):
+                a_sb[c, g] = keep.tile([P, PACK, HALF], F32, name=f"a_sb{c}{g}")
+                f_codes[c, g] = keep.tile([P, HALF], U32, name=f"f_codes{c}{g}", align_bytes=64)
+                f_sc[c, g] = keep.tile([P, HALF], U8, name=f"f_sc{c}{g}", align_bytes=64)
+        h = [[keep.tile([P, S], F32, name=f"h{g}{t}") for t in range(PACK)] for g in range(G)]
+
+        def first_stage(c, g, u):
+            sil = ring3.tile([P, STEP, PACK], F32, name="sil")
+            for i in range(STEP // BLK):
+                n0 = u * STEP + i * BLK
+                acc = psum.tile([P, PACK, BLK], F32, name="acc_a", tag="acc_a")
+                for t in range(PACK):
+                    nc.tensor.matmul_mx(
+                        out=acc[:, t, :],
+                        lhsT=w1_q[g][0][:, t * P : (t + 1) * P].bitcast(FP8X4),
+                        lhsT_scale=w1_q[g][1][:, t * P : (t + 1) * P],
+                        rhs=v_w[c][:, n0 : n0 + BLK].bitcast(FP8X4),
+                        rhs_scale=v_sc[c][:, n0 : n0 + BLK],
+                        start=True,
+                        stop=True,
+                    )
+                nc.scalar.activation(
+                    out=sil[:, i * BLK : (i + 1) * BLK, :], in_=acc[:].rearrange("p t n -> p n t"), func=ACT.Silu
+                )
+                nc.scalar.copy(out=a_sb[c, g][:, :, n0 : n0 + BLK], in_=acc[:])
+            fb = ring3.tile([P, STEP, PACK], BF16, name="fb", align_bytes=64)
+            nc.vector.tensor_tensor(
+                out=fb[:], in0=sil[:], in1=swing_sb[:, g : g + 1, :].to_broadcast([P, STEP, PACK]), op=ALU.mult
+            )
+            f_bf[c, g, u] = fb
+
+        def quantize_f(c, g, u):
+            cols = slice(u * STEP, (u + 1) * STEP)
+            nc.vector.quantize_mx(
+                out=f_codes[c, g][:, cols].bitcast(FP8X4),
+                scales=f_sc[c, g][:, cols],
+                in_=f_bf[c, g, u][:].rearrange("p n t -> p (n t)"),
+            )
+
+        w2_q = []
+
+        def deal_w2(a):
+            words = keep.tile([P, 2 * H], U8, name=f"w2_words{a}", align_bytes=64)
+            nc.vector.tensor_copy(
+                out=words[:].bitcast(U16).rearrange("p (g t m) -> p g t m", g=G, t=PACK),
+                in_=w2_raw[:, a, :].bitcast(U16).rearrange("p (g m t) -> p g t m", g=G, t=PACK),
+            )
+            scales = keep.tile([P, H], U8, name=f"w2_sc{a}", align_bytes=64)
+            nc.vector.tensor_copy(
+                out=scales[:].rearrange("p (g t m) -> p g t m", g=G, t=PACK),
+                in_=w2_sc_raw[:, a, :].rearrange("p (g m t) -> p g t m", g=G, t=PACK),
+            )
+            w2_q.append((words, scales))
+
+        def second_stage(c, g, t):
+            acc = psum.tile([P, HALF], F32, name="acc_b", tag="acc_b")
+            m0 = g * KP + t * P
+            for a in range(G):
+                nc.tensor.matmul_mx(
+                    out=acc[:],
+                    lhsT=w2_q[a][0][:, 2 * m0 : 2 * (m0 + P)].bitcast(FP4X4),
+                    lhsT_scale=w2_q[a][1][:, m0 : m0 + P],
+                    rhs=f_codes[c, a][:].bitcast(FP8X4),
+                    rhs_scale=f_sc[c, a][:],
+                    start=(a == 0),
+                    stop=(a == G - 1),
+                )
+            nc.vector.tensor_tensor(
+                out=h[g][t][:, c * HALF : (c + 1) * HALF], in0=acc[:], in1=a_sb[c, g][:, t, :], op=ALU.max
+            )
+
+        steps = [(c, g, u) for c in range(2) for g in range(G) for u in range(HALF // STEP)]
+        rows = [(g, t) for g in range(G) for t in range(PACK)]
+        w3_raw = []
+        for s, step in enumerate(steps):
+            if s > 0:
+                quantize_f(*steps[s - 1])
+            if s >= 5:
+                for g, t in rows[2 * (s - 5) : 2 * (s - 4)]:
+                    second_stage(0, g, t)
+            first_stage(*step)
+            if s == 0:
+                w1_q.append(w1_operand(1))
+                w3_rows = w3.rearrange("(g p j) n -> g p j n", p=P, j=PACK)
+                for g in range(G):
+                    raw = ring.tile([P, PACK, N], F32, name=f"w3_raw{g}", tag="raw")
+                    nc.sync.dma_start(raw[:], w3_rows[g])
+                    w3_raw.append(raw)
+            if s in (1, 2):
+                deal_w2(s - 1)
+        quantize_f(*steps[-1])
+        for g, t in rows[6:]:
+            second_stage(0, g, t)
+
+        w3_codes = [keep.tile([P, N], U32, name=f"w3_codes{g}", align_bytes=64) for g in range(G)]
+        w3_sc = [keep.tile([P, N], U8, name=f"w3_sc{g}", align_bytes=64) for g in range(G)]
+
+        def w3_operand(g, u):
+            width = N // 2
+            cols = slice(u * width, (u + 1) * width)
+            grouped = ring.tile([P, width, PACK], BF16, name="w3_bf", align_bytes=64)
+            nc.scalar.copy(
+                out=grouped[:].rearrange("p (c i) j -> p c j i", i=4),
+                in_=w3_raw[g][:, :, cols].rearrange("p j (c i) -> p c j i", i=4),
+            )
+            nc.vector.quantize_mx(
+                out=w3_codes[g][:, cols].bitcast(FP8X4),
+                scales=w3_sc[g][:, cols],
+                in_=grouped[:].rearrange("p n j -> p (n j)"),
+            )
+
+        z_codes = {}
+        z_sc = {}
+
+        def pair_sums(g, j0, width, on_vector, with_max):
+            cols = slice(j0 // 16, (j0 + width) // 16)
+            zsum = ring.tile([P, PACK, width], F32, name="zsum")
+            zb = None if on_vector else ring.tile([P, PACK, width], BF16, name="zb")
+            for t in range(PACK):
+                if with_max:
+                    second_stage(1, g, t)
+                one = ring3.tile([P, width], F32, name="one")
+                nc.vector.tensor_copy(one[:], h[g][t][:].indirect(pos1_sb[:, cols]))
+                nc.vector.tensor_tensor(zsum[:, t, :], h[g][t][:].indirect(pos2_sb[:, cols]), one[:], ALU.add)
+                if not on_vector:
+                    nc.scalar.activation(
+                        out=zb[:, t, :], in_=zsum[:, t, :], func=ACT.Copy, scale=panel_sb[:, g, t : t + 1]
+                    )
+            zi = ring.tile([P, width, PACK], BF16, name="zi", align_bytes=64)
+            if on_vector:
+                nc.vector.tensor_tensor(
+                    out=zi[:],
+                    in0=zsum[:].rearrange("p t n -> p n t"),
+                    in1=panel_sb[:, g : g + 1, :].to_broadcast([P, width, PACK]),
+                    op=ALU.mult,
+                )
+            else:
+                nc.scalar.copy(
+                    out=zi[:].rearrange("p (c i) t -> p c t i", i=4),
+                    in_=zb[:].rearrange("p t (c i) -> p c t i", i=4),
+                )
+            return zi
+
+        def quantize_z(g, j0, width, zi):
+            codes = keep.tile([P, width], U32, name=f"z_codes{g}_{j0}", align_bytes=64)
+            scales = keep.tile([P, width], U8, name=f"z_sc{g}_{j0}", align_bytes=64)
+            nc.vector.quantize_mx(
+                out=codes[:].bitcast(FP8X4), scales=scales[:], in_=zi[:].rearrange("p n t -> p (n t)")
+            )
+            return codes, scales
+
+        out_rows = out.rearrange("(k p) j -> p k j", p=P)
+
+        def last_stage(j0, width, z0, z1):
+            per_bank = HALF // width
+            for k0 in range(0, NT, per_bank):
+                kn = min(per_bank, NT - k0)
+                acc = psum.tile([P, kn, width], F32, name="acc_y", tag="acc_a")
+                for k in range(kn):
+                    ncols = slice((k0 + k) * P, (k0 + k + 1) * P)
+                    for g, (codes, scales, lo) in enumerate((z0, z1)):
+                        nc.tensor.matmul_mx(
+                            out=acc[:, k, :],
+                            lhsT=w3_codes[g][:, ncols].bitcast(FP8X4),
+                            lhsT_scale=w3_sc[g][:, ncols],
+                            rhs=codes[:, lo : lo + width].bitcast(FP8X4),
+                            rhs_scale=scales[:, lo : lo + width],
+                            start=(g == 0),
+                            stop=(g == G - 1),
+                        )
+                res = ring3.tile([P, kn, width], F32, name="res")
+                nc.vector.tensor_tensor(
+                    out=res[:], in0=acc[:], in1=base_sb[:, k0 : k0 + kn, j0 : j0 + width], op=ALU.subtract
+                )
+                nc.sync.dma_start(out_rows[:, k0 : k0 + kn, j0 : j0 + width], res[:])
+
+        w3_operand(0, 0)
+        w3_operand(0, 1)
+        base_sb = ring.tile([P, NT, PAIRS], F32, name="base_sb", tag="raw")
+        nc.sync.dma_start(base_sb[:], base.rearrange("(k p) j -> p k j", p=P))
+        zi0 = pair_sums(0, 0, PAIRS, False, True)
+        w3_operand(1, 0)
+        w3_operand(1, 1)
+        pending = None
+        for i, (j0, width) in enumerate(PAIR_CHUNKS):
+            zi = pair_sums(1, j0, width, i == len(PAIR_CHUNKS) - 1, i == 0)
+            if i == 0:
+                z0_codes, z0_sc = quantize_z(0, 0, PAIRS, zi0)
+            else:
+                pj0, pwidth, pzi = pending
+                codes, scales = quantize_z(1, pj0, pwidth, pzi)
+                last_stage(pj0, pwidth, (z0_codes, z0_sc, pj0), (codes, scales, 0))
+            pending = (j0, width, zi)
+        pj0, pwidth, pzi = pending
+        codes, scales = quantize_z(1, pj0, pwidth, pzi)
+        last_stage(pj0, pwidth, (z0_codes, z0_sc, pj0), (codes, scales, 0))

@@ -19,12 +19,39 @@ ALU = mybir.AluOpType
 P = 128
 PACK = 4
 KP = P * PACK
-G = H // KP
-HALF = 512
-BLK = 128
-STEP = 256
-PAIR_CHUNKS = ((0, 256), (256, 128), (384, 128))
+PASSES = H // KP
+BANK = 512
+HALF = S // 2
+BLK = BANK // PACK
+STEP = 2 * BLK
 NT = N // P
+W3_COLS = N // 2
+LINE = 4
+PER_COLUMN = 16
+
+CHUNK_A, CHUNK_B, CHUNK_C = (0, 256), (256, 128), (384, 128)
+ALL_PAIRS = (0, PAIRS)
+
+KIB = 1024
+V_WORDS_AT = 0
+TAB_SC_AT = 3 * KIB
+W1_SECOND_AT = 4 * KIB
+TAB_W_AT = 16 * KIB
+W3_AT = 4 * KIB
+W3_BYTES = PACK * W3_COLS * 4
+W3_LAST_AT = W3_AT + 3 * W3_BYTES
+ZB_ALL_AT = W3_AT + 4 * W3_BYTES
+ZB_A_AT = ZB_ALL_AT + 4 * KIB
+FIRST_AT = ZB_A_AT + 2 * KIB
+ZB_B_AT = FIRST_AT + 4 * KIB
+ZB_C_AT = ZB_B_AT + KIB
+LATE_MAX_AT = ZB_C_AT + KIB
+SILU_AT = {
+    (0, 1, 0): W3_AT + W3_BYTES - 2 * KIB,
+    (0, 1, 1): W3_LAST_AT - 2 * KIB,
+    (1, 1, 1): LATE_MAX_AT + 2 * KIB,
+}
+LATE_ROW_SETS = ((1, 2), (1, 3))
 
 
 def tile_list_mirrored_figure_deviations_kernel(
@@ -35,95 +62,98 @@ def tile_list_mirrored_figure_deviations_kernel(
         keep = ctx.enter_context(tc.tile_pool(name="keep", bufs=1))
         ring = ctx.enter_context(tc.tile_pool(name="ring", bufs=2))
         ring3 = ctx.enter_context(tc.tile_pool(name="ring3", bufs=3))
-        psum = ctx.enter_context(tc.psum_pool(name="psum", bufs=4))
+        shared = ctx.enter_context(tc.tile_pool(name="shared", bufs=1))
+        psum = ctx.enter_context(tc.psum_pool(name="psum", bufs=8))
 
-        offs_sb = keep.tile([P, S // 16], U16, name="offs_sb")
-        pos1_sb = keep.tile([P, PAIRS // 16], U16, name="pos1_sb")
-        pos2_sb = keep.tile([P, PAIRS // 16], U16, name="pos2_sb")
-        swing_sb = keep.tile([P, G, PACK], F32, name="swing_sb")
-        panel_sb = keep.tile([P, G, PACK], F32, name="panel_sb")
-        tab_sc = keep.tile([P, T], U8, name="tab_sc", tag="scale_rows")
-        tab_w = keep.tile([P, T], U32, name="tab_w")
+        offs_sb = keep.tile([P, S // PER_COLUMN], U16, name="offs_sb")
+        pos1_sb = keep.tile([P, PAIRS // PER_COLUMN], U16, name="pos1_sb")
+        pos2_sb = keep.tile([P, PAIRS // PER_COLUMN], U16, name="pos2_sb")
+        tab_sc = shared.tile([P, T], U8, name="tab_sc", offset=TAB_SC_AT, align_bytes=64)
+        tab_w = shared.tile([P, T], U32, name="tab_w", offset=TAB_W_AT, align_bytes=64)
 
-        nc.vector.memset(tab_sc[:].bitcast(I32), 0)
         nc.sync.dma_start(offs_sb[:], offs)
-        sc_rows = tab_scales[0].rearrange("(g r) t -> r g t", r=2)
-        for r in range(2):
-            nc.scalar.dma_start(tab_sc[r:P:16, :].bitcast(I32), sc_rows[r].bitcast(I32))
-        nc.gpsimd.dma_start(swing_sb[:], swing.rearrange("(g p t) -> p g t", p=P, t=PACK))
-        nc.gpsimd.dma_start(panel_sb[:], panel.rearrange("(g p t) -> p g t", p=P, t=PACK))
+        nc.sync.dma_start(
+            tab_sc[:].bitcast(I32), tab_scales[0].bitcast(I32).unsqueeze(1).to_broadcast([16, 8, T // 4])
+        )
         nc.sync.dma_start(pos1_sb[:], pos1)
         nc.sync.dma_start(pos2_sb[:], pos2)
 
-        w1_raw = [ring.tile([P, PACK, KP], F32, name=f"w1_raw{g}", tag="raw") for g in range(G)]
+        w1_raw = [keep.tile([P, PACK, KP], F32, name="w1_raw0", tag="stage")]
         w1_rows = w1.rearrange("(p j) c -> p j c", j=PACK)
-        nc.sync.dma_start(tab_w[:].bitcast(I32), tab_words[0].rearrange("p n t -> p (n t)").bitcast(I32))
         nc.sync.dma_start(w1_raw[0][:], w1_rows[:, :, 0:KP])
+        nc.sync.dma_start(tab_w[:].bitcast(I32), tab_words[0].rearrange("p n t -> p (n t)").bitcast(I32))
+        swing_sb = keep.tile([P, PASSES, PACK], F32, name="swing_sb")
+        nc.sync.dma_start(swing_sb[:], swing.rearrange("(g p t) -> p g t", p=P, t=PACK))
+
+        picked_sc = keep.tile([P, S], U8, name="picked_sc", tag="rows")
+        nc.vector.tensor_copy(picked_sc[:], tab_sc[:].indirect(offs_sb[:]))
+        v_sc = keep.tile([P, S], U8, name="v_sc", align_bytes=64)
+        nc.gpsimd.memset(v_sc[:].bitcast(I32), 0)
+        for r in range(4):
+            nc.sync.dma_start(v_sc[r:P:32, :].bitcast(I32), picked_sc[8 * r : P : 32, :].bitcast(I32))
+
+        w1_raw.append(shared.tile([P, PACK, KP], F32, name="w1_raw1", offset=W1_SECOND_AT, align_bytes=64))
         nc.sync.dma_start(w1_raw[1][:], w1_rows[:, :, KP : 2 * KP])
 
-        v_sc = []
-        for c in range(2):
-            picked = keep.tile([P, HALF], U8, name=f"picked_sc{c}")
-            nc.vector.tensor_copy(picked[:], tab_sc[:].indirect(offs_sb[:, 32 * c : 32 * (c + 1)]))
-            plane = keep.tile([P, HALF], U8, name=f"v_sc{c}", align_bytes=64)
-            nc.vector.tensor_copy(plane[:].bitcast(I32), picked[:].bitcast(I32))
-            for r in range(2):
-                nc.scalar.dma_start(plane[2 + r : P : 32, :].bitcast(I32), picked[16 + r : P : 32, :].bitcast(I32))
-            v_sc.append(plane)
-
-        w2_raw = ring.tile([P, G, 2 * H], U8, name="w2_raw", tag="raw")
-        nc.sync.dma_start(w2_raw[:].bitcast(I32), w2_words.rearrange("a p c -> p a c").bitcast(I32))
-        w2_sc_raw = keep.tile([P, G, H], U8, name="w2_sc_raw", tag="scale_rows")
-        nc.vector.memset(w2_sc_raw[:].bitcast(I32), 0)
-        w2_sc_rows = w2_scales.rearrange("a (q r) c -> r q a c", r=4)
-        for r in range(4):
-            nc.sync.dma_start(w2_sc_raw[r:P:32, :, :].bitcast(I32), w2_sc_rows[r].bitcast(I32))
+        w2_sc_raw = keep.tile([P, H], U8, name="w2_sc_raw", tag="rows")
+        nc.gpsimd.memset(w2_sc_raw[:].bitcast(I32), 0)
+        for d in range(4):
+            nc.sync.dma_start(
+                w2_sc_raw[32 * d : 32 * d + 8, :].bitcast(I32), w2_scales[:, 4 * d : 4 * d + 4, :].bitcast(I32)
+            )
+        w2_sc = [keep.tile([P, H], U8, name=f"w2_sc{a}", align_bytes=64) for a in range(PASSES)]
+        nc.gpsimd.memset(w2_sc[1][:].bitcast(I32), 0)
 
         def w1_operand(g):
             grouped = ring.tile([P, KP * PACK], BF16, name=f"w1_bf{g}", tag="w1_bf", align_bytes=64)
-            dst = grouped[:].rearrange("p (t m j) -> p m j t", t=PACK, j=PACK)
-            src = w1_raw[g][:].rearrange("p j (m t) -> p m j t", t=PACK)
-            if g == 0:
-                nc.scalar.copy(out=dst[:, 0:64], in_=src[:, 0:64])
-                nc.vector.tensor_copy(out=dst[:, 64:128], in_=src[:, 64:128])
-            else:
-                nc.vector.tensor_copy(out=dst, in_=src)
+            nc.vector.tensor_copy(
+                out=grouped[:].rearrange("p (t m j) -> p m t j", t=PACK, j=PACK),
+                in_=w1_raw[g][:].rearrange("p j (m t) -> p m t j", t=PACK),
+            )
             codes = keep.tile([P, KP], U32, name=f"w1_codes{g}", align_bytes=64)
             scales = keep.tile([P, KP], U8, name=f"w1_sc{g}", align_bytes=64)
             nc.vector.quantize_mx(out=codes[:].bitcast(FP8X4), scales=scales[:], in_=grouped[:])
             return codes, scales
 
-        def pick_words(c):
-            words = keep.tile([P, HALF], U32, name=f"v_words{c}", align_bytes=64)
-            nc.vector.tensor_copy(words[:], tab_w[:].indirect(offs_sb[:, 32 * c : 32 * (c + 1)]))
-            return words
+        v_words = shared.tile([P, S], U32, name="v_words", offset=V_WORDS_AT, align_bytes=64)
 
-        v_w = [pick_words(0), pick_words(1)]
+        def pick_words(lo, hi):
+            entries = offs_sb[:, lo // PER_COLUMN : hi // PER_COLUMN]
+            nc.vector.tensor_copy(v_words[:, lo:hi], tab_w[:].indirect(entries))
+
         w1_q = [w1_operand(0)]
+        pick_words(0, STEP)
+        pick_words(STEP, HALF)
+        w2_raw = keep.tile([P, PASSES, 2 * H], U8, name="w2_raw", tag="stage")
+        nc.sync.dma_start(w2_raw[:].bitcast(I32), w2_words.rearrange("a p c -> p a c").bitcast(I32))
 
         a_sb = {}
         f_bf = {}
         f_codes = {}
         f_sc = {}
         for c in range(2):
-            for g in range(G):
+            for g in range(PASSES):
                 a_sb[c, g] = keep.tile([P, PACK, HALF], F32, name=f"a_sb{c}{g}")
                 f_codes[c, g] = keep.tile([P, HALF], U32, name=f"f_codes{c}{g}", align_bytes=64)
                 f_sc[c, g] = keep.tile([P, HALF], U8, name=f"f_sc{c}{g}", align_bytes=64)
-        h = [[keep.tile([P, S], F32, name=f"h{g}{t}") for t in range(PACK)] for g in range(G)]
+        larger = {}
 
         def first_stage(c, g, u):
-            sil = ring3.tile([P, STEP, PACK], F32, name="sil")
+            if (c, g, u) in SILU_AT:
+                sil = shared.tile([P, STEP, PACK], F32, name=f"sil{c}{g}{u}", offset=SILU_AT[c, g, u], align_bytes=64)
+            else:
+                sil = ring3.tile([P, STEP, PACK], F32, name="sil")
             for i in range(STEP // BLK):
                 n0 = u * STEP + i * BLK
-                acc = psum.tile([P, PACK, BLK], F32, name="acc_a", tag="acc_a")
+                figures = slice(c * HALF + n0, c * HALF + n0 + BLK)
+                acc = psum.tile([P, PACK, BLK], F32, name="acc_a", tag="acc")
                 for t in range(PACK):
                     nc.tensor.matmul_mx(
                         out=acc[:, t, :],
                         lhsT=w1_q[g][0][:, t * P : (t + 1) * P].bitcast(FP8X4),
                         lhsT_scale=w1_q[g][1][:, t * P : (t + 1) * P],
-                        rhs=v_w[c][:, n0 : n0 + BLK].bitcast(FP8X4),
-                        rhs_scale=v_sc[c][:, n0 : n0 + BLK],
+                        rhs=v_words[:, figures].bitcast(FP8X4),
+                        rhs_scale=v_sc[:, figures],
                         start=True,
                         stop=True,
                     )
@@ -131,125 +161,156 @@ def tile_list_mirrored_figure_deviations_kernel(
                     out=sil[:, i * BLK : (i + 1) * BLK, :], in_=acc[:].rearrange("p t n -> p n t"), func=ACT.Silu
                 )
                 nc.scalar.copy(out=a_sb[c, g][:, :, n0 : n0 + BLK], in_=acc[:])
-            fb = ring3.tile([P, STEP, PACK], BF16, name="fb", align_bytes=64)
+            if u == 0:
+                f_bf[c, g] = ring.tile([P, HALF, PACK], BF16, name="f_bf", align_bytes=64)
             nc.vector.tensor_tensor(
-                out=fb[:], in0=sil[:], in1=swing_sb[:, g : g + 1, :].to_broadcast([P, STEP, PACK]), op=ALU.mult
+                out=f_bf[c, g][:, u * STEP : (u + 1) * STEP, :],
+                in0=sil[:],
+                in1=swing_sb[:, g : g + 1, :].to_broadcast([P, STEP, PACK]),
+                op=ALU.mult,
             )
-            f_bf[c, g, u] = fb
 
-        def quantize_f(c, g, u):
-            cols = slice(u * STEP, (u + 1) * STEP)
+        def quantize_f(c, g):
             nc.vector.quantize_mx(
-                out=f_codes[c, g][:, cols].bitcast(FP8X4),
-                scales=f_sc[c, g][:, cols],
-                in_=f_bf[c, g, u][:].rearrange("p n t -> p (n t)"),
+                out=f_codes[c, g][:].bitcast(FP8X4),
+                scales=f_sc[c, g][:],
+                in_=f_bf[c, g][:].rearrange("p n t -> p (n t)"),
             )
 
-        w2_q = []
+        w2_codes = []
 
-        def deal_w2(a):
-            words = keep.tile([P, 2 * H], U8, name=f"w2_words{a}", align_bytes=64)
+        def move_w2_words(a):
+            words = keep.tile([P, 2 * H], U8, name=f"w2_codes{a}", align_bytes=64)
             nc.vector.tensor_copy(
-                out=words[:].bitcast(U16).rearrange("p (g t m) -> p g t m", g=G, t=PACK),
-                in_=w2_raw[:, a, :].bitcast(U16).rearrange("p (g m t) -> p g t m", g=G, t=PACK),
+                out=words[:].bitcast(U16).rearrange("p (g t m) -> p g t m", g=PASSES, t=PACK),
+                in_=w2_raw[:, a, :].bitcast(U16).rearrange("p (g m t) -> p g t m", g=PASSES, t=PACK),
             )
-            scales = keep.tile([P, H], U8, name=f"w2_sc{a}", align_bytes=64)
+            w2_codes.append(words)
+
+        def move_w2_scales():
             nc.vector.tensor_copy(
-                out=scales[:].rearrange("p (g t m) -> p g t m", g=G, t=PACK),
-                in_=w2_sc_raw[:, a, :].rearrange("p (g m t) -> p g t m", g=G, t=PACK),
+                out=w2_sc[0][:].rearrange("p (g t m) -> p g t m", g=PASSES, t=PACK),
+                in_=w2_sc_raw[:].rearrange("p (g m t) -> p g t m", g=PASSES, t=PACK),
             )
-            w2_q.append((words, scales))
+            for d in range(4):
+                nc.sync.dma_start(
+                    w2_sc[1][32 * d : 32 * d + 4, :].bitcast(I32), w2_sc[0][32 * d + 4 : 32 * d + 8, :].bitcast(I32)
+                )
 
         def second_stage(c, g, t):
-            acc = psum.tile([P, HALF], F32, name="acc_b", tag="acc_b")
+            if c == 0 and (g, t) in LATE_ROW_SETS:
+                place = LATE_MAX_AT + LATE_ROW_SETS.index((g, t)) * S * 4
+                larger[g, t] = shared.tile([P, S], F32, name=f"larger{g}{t}", offset=place, align_bytes=64)
+            elif c == 0:
+                larger[g, t] = keep.tile([P, S], F32, name=f"larger{g}{t}")
+            acc = psum.tile([P, HALF], F32, name="acc_b", tag="acc")
             m0 = g * KP + t * P
-            for a in range(G):
+            for a in range(PASSES):
                 nc.tensor.matmul_mx(
                     out=acc[:],
-                    lhsT=w2_q[a][0][:, 2 * m0 : 2 * (m0 + P)].bitcast(FP4X4),
-                    lhsT_scale=w2_q[a][1][:, m0 : m0 + P],
+                    lhsT=w2_codes[a][:, 2 * m0 : 2 * (m0 + P)].bitcast(FP4X4),
+                    lhsT_scale=w2_sc[a][:, m0 : m0 + P],
                     rhs=f_codes[c, a][:].bitcast(FP8X4),
                     rhs_scale=f_sc[c, a][:],
                     start=(a == 0),
-                    stop=(a == G - 1),
+                    stop=(a == PASSES - 1),
                 )
             nc.vector.tensor_tensor(
-                out=h[g][t][:, c * HALF : (c + 1) * HALF], in0=acc[:], in1=a_sb[c, g][:, t, :], op=ALU.max
+                out=larger[g, t][:, c * HALF : (c + 1) * HALF], in0=acc[:], in1=a_sb[c, g][:, t, :], op=ALU.max
             )
 
-        steps = [(c, g, u) for c in range(2) for g in range(G) for u in range(HALF // STEP)]
-        rows = [(g, t) for g in range(G) for t in range(PACK)]
-        w3_raw = []
-        for s, step in enumerate(steps):
-            if s > 0:
-                quantize_f(*steps[s - 1])
-            if s >= 5:
-                for g, t in rows[2 * (s - 5) : 2 * (s - 4)]:
-                    second_stage(0, g, t)
-            first_stage(*step)
-            if s == 0:
-                w1_q.append(w1_operand(1))
-                w3_rows = w3.rearrange("(g p j) n -> g p j n", p=P, j=PACK)
-                for g in range(G):
-                    raw = ring.tile([P, PACK, N], F32, name=f"w3_raw{g}", tag="raw")
-                    nc.sync.dma_start(raw[:], w3_rows[g])
-                    w3_raw.append(raw)
-            if s in (1, 2):
-                deal_w2(s - 1)
-        quantize_f(*steps[-1])
-        for g, t in rows[6:]:
-            second_stage(0, g, t)
+        first_stage(0, 0, 0)
+        w1_q.append(w1_operand(1))
+        first_stage(0, 0, 1)
+        move_w2_scales()
+        pick_words(HALF, S)
+        quantize_f(0, 0)
+        first_stage(0, 1, 0)
+        move_w2_words(0)
+        first_stage(0, 1, 1)
+        move_w2_words(1)
 
-        w3_codes = [keep.tile([P, N], U32, name=f"w3_codes{g}", align_bytes=64) for g in range(G)]
-        w3_sc = [keep.tile([P, N], U8, name=f"w3_sc{g}", align_bytes=64) for g in range(G)]
-
-        def w3_operand(g, u):
-            width = N // 2
-            cols = slice(u * width, (u + 1) * width)
-            grouped = ring.tile([P, width, PACK], BF16, name="w3_bf", align_bytes=64)
-            nc.scalar.copy(
-                out=grouped[:].rearrange("p (c i) j -> p c j i", i=4),
-                in_=w3_raw[g][:, :, cols].rearrange("p j (c i) -> p c j i", i=4),
-            )
-            nc.vector.quantize_mx(
-                out=w3_codes[g][:, cols].bitcast(FP8X4),
-                scales=w3_sc[g][:, cols],
-                in_=grouped[:].rearrange("p n j -> p (n j)"),
-            )
-
-        z_codes = {}
-        z_sc = {}
-
-        def pair_sums(g, j0, width, on_vector, with_max):
-            cols = slice(j0 // 16, (j0 + width) // 16)
-            zsum = ring.tile([P, PACK, width], F32, name="zsum")
-            zb = None if on_vector else ring.tile([P, PACK, width], BF16, name="zb")
-            for t in range(PACK):
-                if with_max:
-                    second_stage(1, g, t)
-                one = ring3.tile([P, width], F32, name="one")
-                nc.vector.tensor_copy(one[:], h[g][t][:].indirect(pos1_sb[:, cols]))
-                nc.vector.tensor_tensor(zsum[:, t, :], h[g][t][:].indirect(pos2_sb[:, cols]), one[:], ALU.add)
-                if not on_vector:
-                    nc.scalar.activation(
-                        out=zb[:, t, :], in_=zsum[:, t, :], func=ACT.Copy, scale=panel_sb[:, g, t : t + 1]
-                    )
-            zi = ring.tile([P, width, PACK], BF16, name="zi", align_bytes=64)
-            if on_vector:
-                nc.vector.tensor_tensor(
-                    out=zi[:],
-                    in0=zsum[:].rearrange("p t n -> p n t"),
-                    in1=panel_sb[:, g : g + 1, :].to_broadcast([P, width, PACK]),
-                    op=ALU.mult,
+        panel_sb = keep.tile([P, PASSES, PACK], F32, name="panel_sb", tag="rows")
+        nc.sync.dma_start(panel_sb[:], panel.rearrange("(g p t) -> p g t", p=P, t=PACK))
+        w3_rows = w3.rearrange("(g p j) n -> g p j n", p=P, j=PACK)
+        w3_raw = {}
+        for g in range(PASSES):
+            for u in range(2):
+                place = W3_AT + (2 * g + u) * W3_BYTES
+                w3_raw[g, u] = shared.tile(
+                    [P, PACK, W3_COLS], F32, name=f"w3_raw{g}{u}", offset=place, align_bytes=64
                 )
-            else:
+                nc.sync.dma_start(w3_raw[g, u][:], w3_rows[g][:, :, u * W3_COLS : (u + 1) * W3_COLS])
+        base_sb = keep.tile([P, NT, PAIRS], F32, name="base_sb", tag="stage")
+        nc.sync.dma_start(base_sb[:], base.rearrange("(k p) j -> p k j", p=P))
+
+        quantize_f(0, 1)
+        first_stage(1, 0, 0)
+        second_stage(0, 0, 0)
+        second_stage(0, 0, 1)
+        first_stage(1, 0, 1)
+        quantize_f(1, 0)
+        second_stage(0, 0, 2)
+        second_stage(0, 0, 3)
+        first_stage(1, 1, 0)
+        second_stage(0, 1, 0)
+        second_stage(0, 1, 1)
+        first_stage(1, 1, 1)
+        quantize_f(1, 1)
+        second_stage(0, 1, 2)
+        second_stage(0, 1, 3)
+
+        w3_codes = [keep.tile([P, N], U32, name=f"w3_codes{g}", align_bytes=64) for g in range(PASSES)]
+        w3_sc = [keep.tile([P, N], U8, name=f"w3_sc{g}", align_bytes=64) for g in range(PASSES)]
+        for g in range(PASSES):
+            for u in range(2):
+                cols = slice(u * W3_COLS, (u + 1) * W3_COLS)
+                w3_bf = ring.tile([P, W3_COLS, PACK], BF16, name="w3_bf", align_bytes=64)
                 nc.scalar.copy(
-                    out=zi[:].rearrange("p (c i) t -> p c t i", i=4),
-                    in_=zb[:].rearrange("p t (c i) -> p c t i", i=4),
+                    out=w3_bf[:].rearrange("p (c i) j -> p c j i", i=LINE),
+                    in_=w3_raw[g, u][:].rearrange("p j (c i) -> p c j i", i=LINE),
                 )
+                nc.vector.quantize_mx(
+                    out=w3_codes[g][:, cols].bitcast(FP8X4),
+                    scales=w3_sc[g][:, cols],
+                    in_=w3_bf[:].rearrange("p n j -> p (n j)"),
+                )
+
+        zsum = {}
+        zb = {}
+        for g, chunk, place in (
+            (0, ALL_PAIRS, ZB_ALL_AT),
+            (1, CHUNK_A, ZB_A_AT),
+            (1, CHUNK_B, ZB_B_AT),
+            (1, CHUNK_C, ZB_C_AT),
+        ):
+            j0, width = chunk
+            zsum[g, chunk] = keep.tile([P, PACK, width], F32, name=f"zsum{g}_{j0}")
+            zb[g, chunk] = shared.tile([P, PACK, width], BF16, name=f"zb{g}_{j0}", offset=place, align_bytes=64)
+
+        def pair_sums(g, chunk, t0, place):
+            j0, width = chunk
+            cols = slice(j0 // PER_COLUMN, (j0 + width) // PER_COLUMN)
+            first = shared.tile([P, 2, width], F32, name=f"first{g}_{j0}_{t0}", offset=place, align_bytes=64)
+            for t in (t0, t0 + 1):
+                nc.vector.tensor_copy(first[:, t - t0, :], larger[g, t][:].indirect(pos1_sb[:, cols]))
+            for t in (t0, t0 + 1):
+                sums = zsum[g, chunk][:, t, :]
+                nc.vector.tensor_tensor(sums, larger[g, t][:].indirect(pos2_sb[:, cols]), first[:, t - t0, :], ALU.add)
+                nc.scalar.activation(
+                    out=zb[g, chunk][:, t, :], in_=sums, func=ACT.Copy, scale=panel_sb[:, g, t : t + 1]
+                )
+
+        def interleave(g, chunk):
+            zi = ring3.tile([P, chunk[1], PACK], BF16, name="zi", align_bytes=64)
+            nc.scalar.copy(
+                out=zi[:].rearrange("p (c i) t -> p c t i", i=LINE),
+                in_=zb[g, chunk][:].rearrange("p t (c i) -> p c t i", i=LINE),
+            )
             return zi
 
-        def quantize_z(g, j0, width, zi):
+        def quantize_z(g, chunk, zi):
+            j0, width = chunk
             codes = keep.tile([P, width], U32, name=f"z_codes{g}_{j0}", align_bytes=64)
             scales = keep.tile([P, width], U8, name=f"z_sc{g}_{j0}", align_bytes=64)
             nc.vector.quantize_mx(
@@ -259,46 +320,52 @@ def tile_list_mirrored_figure_deviations_kernel(
 
         out_rows = out.rearrange("(k p) j -> p k j", p=P)
 
-        def last_stage(j0, width, z0, z1):
-            per_bank = HALF // width
+        def last_stage(chunk, z_all, z_chunk):
+            j0, width = chunk
+            per_bank = BANK // width
             for k0 in range(0, NT, per_bank):
                 kn = min(per_bank, NT - k0)
-                acc = psum.tile([P, kn, width], F32, name="acc_y", tag="acc_a")
-                for k in range(kn):
-                    ncols = slice((k0 + k) * P, (k0 + k + 1) * P)
-                    for g, (codes, scales, lo) in enumerate((z0, z1)):
+                acc = psum.tile([P, kn, width], F32, name="acc_y", tag="acc")
+                for g, (codes, scales, lo) in enumerate(((*z_all, j0), (*z_chunk, 0))):
+                    for k in range(kn):
+                        ncols = slice((k0 + k) * P, (k0 + k + 1) * P)
                         nc.tensor.matmul_mx(
                             out=acc[:, k, :],
                             lhsT=w3_codes[g][:, ncols].bitcast(FP8X4),
                             lhsT_scale=w3_sc[g][:, ncols],
                             rhs=codes[:, lo : lo + width].bitcast(FP8X4),
                             rhs_scale=scales[:, lo : lo + width],
-                            start=(g == 0),
-                            stop=(g == G - 1),
+                            start=(g == 0 and k == 0),
+                            stop=(g == PASSES - 1 and k == kn - 1),
                         )
-                res = ring3.tile([P, kn, width], F32, name="res")
+                res = keep.tile([P, kn, width], F32, name=f"res{j0}_{k0}")
                 nc.vector.tensor_tensor(
                     out=res[:], in0=acc[:], in1=base_sb[:, k0 : k0 + kn, j0 : j0 + width], op=ALU.subtract
                 )
                 nc.sync.dma_start(out_rows[:, k0 : k0 + kn, j0 : j0 + width], res[:])
 
-        w3_operand(0, 0)
-        w3_operand(0, 1)
-        base_sb = ring.tile([P, NT, PAIRS], F32, name="base_sb", tag="raw")
-        nc.sync.dma_start(base_sb[:], base.rearrange("(k p) j -> p k j", p=P))
-        zi0 = pair_sums(0, 0, PAIRS, False, True)
-        w3_operand(1, 0)
-        w3_operand(1, 1)
-        pending = None
-        for i, (j0, width) in enumerate(PAIR_CHUNKS):
-            zi = pair_sums(1, j0, width, i == len(PAIR_CHUNKS) - 1, i == 0)
-            if i == 0:
-                z0_codes, z0_sc = quantize_z(0, 0, PAIRS, zi0)
-            else:
-                pj0, pwidth, pzi = pending
-                codes, scales = quantize_z(1, pj0, pwidth, pzi)
-                last_stage(pj0, pwidth, (z0_codes, z0_sc, pj0), (codes, scales, 0))
-            pending = (j0, width, zi)
-        pj0, pwidth, pzi = pending
-        codes, scales = quantize_z(1, pj0, pwidth, pzi)
-        last_stage(pj0, pwidth, (z0_codes, z0_sc, pj0), (codes, scales, 0))
+        second_stage(1, 0, 0)
+        second_stage(1, 0, 1)
+        pair_sums(0, ALL_PAIRS, 0, FIRST_AT)
+        second_stage(1, 0, 2)
+        second_stage(1, 0, 3)
+        pair_sums(0, ALL_PAIRS, 2, W3_LAST_AT - KIB)
+        zi_all = interleave(0, ALL_PAIRS)
+        for t in range(PACK):
+            second_stage(1, 1, t)
+        pair_sums(1, CHUNK_A, 0, W3_LAST_AT + 3 * KIB)
+        pair_sums(1, CHUNK_B, 0, W3_LAST_AT + 5 * KIB)
+        z_all = quantize_z(0, ALL_PAIRS, zi_all)
+        pair_sums(1, CHUNK_A, 2, ZB_ALL_AT)
+        zi_a = interleave(1, CHUNK_A)
+        pair_sums(1, CHUNK_B, 2, ZB_ALL_AT + 2 * KIB)
+        zi_b = interleave(1, CHUNK_B)
+        pair_sums(1, CHUNK_C, 0, ZB_ALL_AT + 3 * KIB)
+        z_a = quantize_z(1, CHUNK_A, zi_a)
+        pair_sums(1, CHUNK_C, 2, ZB_A_AT)
+        zi_c = interleave(1, CHUNK_C)
+        z_b = quantize_z(1, CHUNK_B, zi_b)
+        last_stage(CHUNK_A, z_all, z_a)
+        z_c = quantize_z(1, CHUNK_C, zi_c)
+        last_stage(CHUNK_B, z_all, z_b)
+        last_stage(CHUNK_C, z_all, z_c)

from contextlib import ExitStack

import concourse.mybir as mybir

T, S, PAIRS, K, H, N = 2048, 1024, 512, 512, 1024, 768
FLOPS = 2 * (K * H * S + H * H * S + H * N * PAIRS)

F32 = mybir.dt.float32
BF16 = mybir.dt.bfloat16
I32 = mybir.dt.int32
U32 = mybir.dt.uint32
U16 = mybir.dt.uint16
U8 = mybir.dt.uint8
FP8X4 = mybir.dt.float8_e4m3fn_x4
FP4X4 = mybir.dt.float4_e2m1fn_x4
ACT = mybir.ActivationFunctionType
ALU = mybir.AluOpType

P = 128
PACK = 4
KP = P * PACK
PASSES = H // KP
BANK = 512
HALF = S // 2
BLK = BANK // PACK
STEP = 2 * BLK
NT = N // P
W3_COLS = N // 2
LINE = 4
PER_COLUMN = 16

CHUNK_A, CHUNK_B, CHUNK_C = (0, 256), (256, 128), (384, 128)
ALL_PAIRS = (0, PAIRS)

KIB = 1024
V_WORDS_AT = 0
TAB_SC_AT = 3 * KIB
W1_SECOND_AT = 4 * KIB
TAB_W_AT = 16 * KIB
W3_AT = 4 * KIB
W3_BYTES = PACK * W3_COLS * 4
W3_LAST_AT = W3_AT + 3 * W3_BYTES
ZB_ALL_AT = W3_AT + 4 * W3_BYTES
ZB_A_AT = ZB_ALL_AT + 4 * KIB
FIRST_AT = ZB_A_AT + 2 * KIB
ZB_B_AT = FIRST_AT + 4 * KIB
ZB_C_AT = ZB_B_AT + KIB
LATE_MAX_AT = ZB_C_AT + KIB
SILU_AT = {
    (0, 1, 0): W3_AT + W3_BYTES - 2 * KIB,
    (0, 1, 1): W3_LAST_AT - 2 * KIB,
    (1, 1, 1): LATE_MAX_AT + 2 * KIB,
}
LATE_ROW_SETS = ((1, 2), (1, 3))


def tile_list_mirrored_figure_deviations_kernel(
    tc, tab_words, tab_scales, offs, pos1, pos2, w1, swing, w2_words, w2_scales, panel, w3, base, out
):
    nc = tc.nc
    with ExitStack() as ctx:
        keep = ctx.enter_context(tc.tile_pool(name="keep", bufs=1))
        ring = ctx.enter_context(tc.tile_pool(name="ring", bufs=2))
        ring3 = ctx.enter_context(tc.tile_pool(name="ring3", bufs=3))
        shared = ctx.enter_context(tc.tile_pool(name="shared", bufs=1))
        psum = ctx.enter_context(tc.psum_pool(name="psum", bufs=8))

        offs_sb = keep.tile([P, S // PER_COLUMN], U16, name="offs_sb")
        pos1_sb = keep.tile([P, PAIRS // PER_COLUMN], U16, name="pos1_sb")
        pos2_sb = keep.tile([P, PAIRS // PER_COLUMN], U16, name="pos2_sb")
        tab_sc = shared.tile([P, T], U8, name="tab_sc", offset=TAB_SC_AT, align_bytes=64)
        tab_w = shared.tile([P, T], U32, name="tab_w", offset=TAB_W_AT, align_bytes=64)

        nc.sync.dma_start(offs_sb[:], offs)
        nc.sync.dma_start(
            tab_sc[:].bitcast(I32), tab_scales[0].bitcast(I32).unsqueeze(1).to_broadcast([16, 8, T // 4])
        )
        nc.sync.dma_start(pos1_sb[:], pos1)
        nc.sync.dma_start(pos2_sb[:], pos2)

        w1_raw = [keep.tile([P, PACK, KP], F32, name="w1_raw0", tag="stage")]
        w1_rows = w1.rearrange("(p j) c -> p j c", j=PACK)
        nc.sync.dma_start(w1_raw[0][:], w1_rows[:, :, 0:KP])
        nc.sync.dma_start(tab_w[:].bitcast(I32), tab_words[0].rearrange("p n t -> p (n t)").bitcast(I32))
        swing_sb = keep.tile([P, PASSES, PACK], F32, name="swing_sb")
        nc.sync.dma_start(swing_sb[:], swing.rearrange("(g p t) -> p g t", p=P, t=PACK))

        picked_sc = keep.tile([P, S], U8, name="picked_sc", tag="rows")
        nc.vector.tensor_copy(picked_sc[:], tab_sc[:].indirect(offs_sb[:]))
        v_sc = keep.tile([P, S], U8, name="v_sc", align_bytes=64)
        nc.gpsimd.memset(v_sc[:].bitcast(I32), 0)
        for r in range(4):
            nc.sync.dma_start(v_sc[r:P:32, :].bitcast(I32), picked_sc[8 * r : P : 32, :].bitcast(I32))

        w1_raw.append(shared.tile([P, PACK, KP], F32, name="w1_raw1", offset=W1_SECOND_AT, align_bytes=64))
        nc.sync.dma_start(w1_raw[1][:], w1_rows[:, :, KP : 2 * KP])

        w2_sc_raw = keep.tile([P, H], U8, name="w2_sc_raw", tag="rows")
        nc.gpsimd.memset(w2_sc_raw[:].bitcast(I32), 0)
        for d in range(4):
            nc.sync.dma_start(
                w2_sc_raw[32 * d : 32 * d + 8, :].bitcast(I32), w2_scales[:, 4 * d : 4 * d + 4, :].bitcast(I32)
            )
        w2_sc = [keep.tile([P, H], U8, name=f"w2_sc{a}", align_bytes=64) for a in range(PASSES)]
        nc.gpsimd.memset(w2_sc[1][:].bitcast(I32), 0)

        def w1_operand(g):
            grouped = ring.tile([P, KP * PACK], BF16, name=f"w1_bf{g}", tag="w1_bf", align_bytes=64)
            nc.vector.tensor_copy(
                out=grouped[:].rearrange("p (t m j) -> p m t j", t=PACK, j=PACK),
                in_=w1_raw[g][:].rearrange("p j (m t) -> p m t j", t=PACK),
            )
            codes = keep.tile([P, KP], U32, name=f"w1_codes{g}", align_bytes=64)
            scales = keep.tile([P, KP], U8, name=f"w1_sc{g}", align_bytes=64)
            nc.vector.quantize_mx(out=codes[:].bitcast(FP8X4), scales=scales[:], in_=grouped[:])
            return codes, scales

        v_words = shared.tile([P, S], U32, name="v_words", offset=V_WORDS_AT, align_bytes=64)

        def pick_words(lo, hi):
            entries = offs_sb[:, lo // PER_COLUMN : hi // PER_COLUMN]
            nc.vector.tensor_copy(v_words[:, lo:hi], tab_w[:].indirect(entries))

        w1_q = [w1_operand(0)]
        pick_words(0, STEP)
        pick_words(STEP, HALF)
        w2_raw = keep.tile([P, PASSES, 2 * H], U8, name="w2_raw", tag="stage")
        nc.sync.dma_start(w2_raw[:].bitcast(I32), w2_words.rearrange("a p c -> p a c").bitcast(I32))

        a_sb = {}
        f_bf = {}
        f_codes = {}
        f_sc = {}
        for c in range(2):
            for g in range(PASSES):
                a_sb[c, g] = keep.tile([P, PACK, HALF], F32, name=f"a_sb{c}{g}")
                f_codes[c, g] = keep.tile([P, HALF], U32, name=f"f_codes{c}{g}", align_bytes=64)
                f_sc[c, g] = keep.tile([P, HALF], U8, name=f"f_sc{c}{g}", align_bytes=64)
        larger = {}

        def first_stage(c, g, u):
            if (c, g, u) in SILU_AT:
                sil = shared.tile([P, STEP, PACK], F32, name=f"sil{c}{g}{u}", offset=SILU_AT[c, g, u], align_bytes=64)
            else:
                sil = ring3.tile([P, STEP, PACK], F32, name="sil")
            for i in range(STEP // BLK):
                n0 = u * STEP + i * BLK
                figures = slice(c * HALF + n0, c * HALF + n0 + BLK)
                acc = psum.tile([P, PACK, BLK], F32, name="acc_a", tag="acc")
                for t in range(PACK):
                    nc.tensor.matmul_mx(
                        out=acc[:, t, :],
                        lhsT=w1_q[g][0][:, t * P : (t + 1) * P].bitcast(FP8X4),
                        lhsT_scale=w1_q[g][1][:, t * P : (t + 1) * P],
                        rhs=v_words[:, figures].bitcast(FP8X4),
                        rhs_scale=v_sc[:, figures],
                        start=True,
                        stop=True,
                    )
                nc.scalar.activation(
                    out=sil[:, i * BLK : (i + 1) * BLK, :], in_=acc[:].rearrange("p t n -> p n t"), func=ACT.Silu
                )
                nc.scalar.copy(out=a_sb[c, g][:, :, n0 : n0 + BLK], in_=acc[:])
            if u == 0:
                f_bf[c, g] = ring.tile([P, HALF, PACK], BF16, name="f_bf", align_bytes=64)
            nc.vector.tensor_tensor(
                out=f_bf[c, g][:, u * STEP : (u + 1) * STEP, :],
                in0=sil[:],
                in1=swing_sb[:, g : g + 1, :].to_broadcast([P, STEP, PACK]),
                op=ALU.mult,
            )

        def quantize_f(c, g):
            nc.vector.quantize_mx(
                out=f_codes[c, g][:].bitcast(FP8X4),
                scales=f_sc[c, g][:],
                in_=f_bf[c, g][:].rearrange("p n t -> p (n t)"),
            )

        w2_codes = []

        def move_w2_words(a):
            words = keep.tile([P, 2 * H], U8, name=f"w2_codes{a}", align_bytes=64)
            nc.vector.tensor_copy(
                out=words[:].bitcast(U16).rearrange("p (g t m) -> p g t m", g=PASSES, t=PACK),
                in_=w2_raw[:, a, :].bitcast(U16).rearrange("p (g m t) -> p g t m", g=PASSES, t=PACK),
            )
            w2_codes.append(words)

        def move_w2_scales():
            nc.vector.tensor_copy(
                out=w2_sc[0][:].rearrange("p (g t m) -> p g t m", g=PASSES, t=PACK),
                in_=w2_sc_raw[:].rearrange("p (g m t) -> p g t m", g=PASSES, t=PACK),
            )
            for d in range(4):
                nc.sync.dma_start(
                    w2_sc[1][32 * d : 32 * d + 4, :].bitcast(I32), w2_sc[0][32 * d + 4 : 32 * d + 8, :].bitcast(I32)
                )

        def second_stage(c, g, t):
            if c == 0 and (g, t) in LATE_ROW_SETS:
                place = LATE_MAX_AT + LATE_ROW_SETS.index((g, t)) * S * 4
                larger[g, t] = shared.tile([P, S], F32, name=f"larger{g}{t}", offset=place, align_bytes=64)
            elif c == 0:
                larger[g, t] = keep.tile([P, S], F32, name=f"larger{g}{t}")
            acc = psum.tile([P, HALF], F32, name="acc_b", tag="acc")
            m0 = g * KP + t * P
            for a in range(PASSES):
                nc.tensor.matmul_mx(
                    out=acc[:],
                    lhsT=w2_codes[a][:, 2 * m0 : 2 * (m0 + P)].bitcast(FP4X4),
                    lhsT_scale=w2_sc[a][:, m0 : m0 + P],
                    rhs=f_codes[c, a][:].bitcast(FP8X4),
                    rhs_scale=f_sc[c, a][:],
                    start=(a == 0),
                    stop=(a == PASSES - 1),
                )
            nc.vector.tensor_tensor(
                out=larger[g, t][:, c * HALF : (c + 1) * HALF], in0=acc[:], in1=a_sb[c, g][:, t, :], op=ALU.max
            )

        first_stage(0, 0, 0)
        w1_q.append(w1_operand(1))
        first_stage(0, 0, 1)
        move_w2_scales()
        pick_words(HALF, S)
        quantize_f(0, 0)
        first_stage(0, 1, 0)
        move_w2_words(0)
        first_stage(0, 1, 1)
        move_w2_words(1)

        panel_sb = keep.tile([P, PASSES, PACK], F32, name="panel_sb", tag="rows")
        nc.sync.dma_start(panel_sb[:], panel.rearrange("(g p t) -> p g t", p=P, t=PACK))
        w3_rows = w3.rearrange("(g p j) n -> g p j n", p=P, j=PACK)
        w3_raw = {}
        for g in range(PASSES):
            for u in range(2):
                place = W3_AT + (2 * g + u) * W3_BYTES
                w3_raw[g, u] = shared.tile(
                    [P, PACK, W3_COLS], F32, name=f"w3_raw{g}{u}", offset=place, align_bytes=64
                )
                nc.sync.dma_start(w3_raw[g, u][:], w3_rows[g][:, :, u * W3_COLS : (u + 1) * W3_COLS])
        base_sb = keep.tile([P, NT, PAIRS], F32, name="base_sb", tag="stage")
        nc.sync.dma_start(base_sb[:], base.rearrange("(k p) j -> p k j", p=P))

        quantize_f(0, 1)
        first_stage(1, 0, 0)
        second_stage(0, 0, 0)
        second_stage(0, 0, 1)
        first_stage(1, 0, 1)
        quantize_f(1, 0)
        second_stage(0, 0, 2)
        second_stage(0, 0, 3)
        first_stage(1, 1, 0)
        second_stage(0, 1, 0)
        second_stage(0, 1, 1)
        first_stage(1, 1, 1)
        quantize_f(1, 1)
        second_stage(0, 1, 2)
        second_stage(0, 1, 3)

        w3_codes = [keep.tile([P, N], U32, name=f"w3_codes{g}", align_bytes=64) for g in range(PASSES)]
        w3_sc = [keep.tile([P, N], U8, name=f"w3_sc{g}", align_bytes=64) for g in range(PASSES)]
        for g in range(PASSES):
            for u in range(2):
                cols = slice(u * W3_COLS, (u + 1) * W3_COLS)
                w3_bf = ring.tile([P, W3_COLS, PACK], BF16, name="w3_bf", align_bytes=64)
                nc.scalar.copy(
                    out=w3_bf[:].rearrange("p (c i) j -> p c j i", i=LINE),
                    in_=w3_raw[g, u][:].rearrange("p j (c i) -> p c j i", i=LINE),
                )
                nc.vector.quantize_mx(
                    out=w3_codes[g][:, cols].bitcast(FP8X4),
                    scales=w3_sc[g][:, cols],
                    in_=w3_bf[:].rearrange("p n j -> p (n j)"),
                )

        zsum = {}
        zb = {}
        for g, chunk, place in (
            (0, ALL_PAIRS, ZB_ALL_AT),
            (1, CHUNK_A, ZB_A_AT),
            (1, CHUNK_B, ZB_B_AT),
            (1, CHUNK_C, ZB_C_AT),
        ):
            j0, width = chunk
            zsum[g, chunk] = keep.tile([P, PACK, width], F32, name=f"zsum{g}_{j0}")
            zb[g, chunk] = shared.tile([P, PACK, width], BF16, name=f"zb{g}_{j0}", offset=place, align_bytes=64)

        def pair_sums(g, chunk, t0, place):
            j0, width = chunk
            cols = slice(j0 // PER_COLUMN, (j0 + width) // PER_COLUMN)
            first = shared.tile([P, 2, width], F32, name=f"first{g}_{j0}_{t0}", offset=place, align_bytes=64)
            for t in (t0, t0 + 1):
                nc.vector.tensor_copy(first[:, t - t0, :], larger[g, t][:].indirect(pos1_sb[:, cols]))
            for t in (t0, t0 + 1):
                sums = zsum[g, chunk][:, t, :]
                nc.vector.tensor_tensor(sums, larger[g, t][:].indirect(pos2_sb[:, cols]), first[:, t - t0, :], ALU.add)
                nc.scalar.activation(
                    out=zb[g, chunk][:, t, :], in_=sums, func=ACT.Copy, scale=panel_sb[:, g, t : t + 1]
                )

        def interleave(g, chunk):
            zi = ring3.tile([P, chunk[1], PACK], BF16, name="zi", align_bytes=64)
            nc.scalar.copy(
                out=zi[:].rearrange("p (c i) t -> p c t i", i=LINE),
                in_=zb[g, chunk][:].rearrange("p t (c i) -> p c t i", i=LINE),
            )
            return zi

        def quantize_z(g, chunk, zi):
            j0, width = chunk
            codes = keep.tile([P, width], U32, name=f"z_codes{g}_{j0}", align_bytes=64)
            scales = keep.tile([P, width], U8, name=f"z_sc{g}_{j0}", align_bytes=64)
            nc.vector.quantize_mx(
                out=codes[:].bitcast(FP8X4), scales=scales[:], in_=zi[:].rearrange("p n t -> p (n t)")
            )
            return codes, scales

        out_rows = out.rearrange("(k p) j -> p k j", p=P)

        def last_stage(chunk, z_all, z_chunk):
            j0, width = chunk
            per_bank = BANK // width
            for k0 in range(0, NT, per_bank):
                kn = min(per_bank, NT - k0)
                acc = psum.tile([P, kn, width], F32, name="acc_y", tag="acc")
                for g, (codes, scales, lo) in enumerate(((*z_all, j0), (*z_chunk, 0))):
                    for k in range(kn):
                        ncols = slice((k0 + k) * P, (k0 + k + 1) * P)
                        nc.tensor.matmul_mx(
                            out=acc[:, k, :],
                            lhsT=w3_codes[g][:, ncols].bitcast(FP8X4),
                            lhsT_scale=w3_sc[g][:, ncols],
                            rhs=codes[:, lo : lo + width].bitcast(FP8X4),
                            rhs_scale=scales[:, lo : lo + width],
                            start=(g == 0 and k == 0),
                            stop=(g == PASSES - 1 and k == kn - 1),
                        )
                res = keep.tile([P, kn, width], F32, name=f"res{j0}_{k0}")
                nc.vector.tensor_tensor(
                    out=res[:], in0=acc[:], in1=base_sb[:, k0 : k0 + kn, j0 : j0 + width], op=ALU.subtract
                )
                nc.sync.dma_start(out_rows[:, k0 : k0 + kn, j0 : j0 + width], res[:])

        second_stage(1, 0, 0)
        second_stage(1, 0, 1)
        pair_sums(0, ALL_PAIRS, 0, FIRST_AT)
        second_stage(1, 0, 2)
        second_stage(1, 0, 3)
        pair_sums(0, ALL_PAIRS, 2, W3_LAST_AT - KIB)
        zi_all = interleave(0, ALL_PAIRS)
        for t in range(PACK):
            second_stage(1, 1, t)
        pair_sums(1, CHUNK_A, 0, W3_LAST_AT + 3 * KIB)
        pair_sums(1, CHUNK_B, 0, W3_LAST_AT + 5 * KIB)
        z_all = quantize_z(0, ALL_PAIRS, zi_all)
        pair_sums(1, CHUNK_A, 2, ZB_ALL_AT)
        zi_a = interleave(1, CHUNK_A)
        pair_sums(1, CHUNK_B, 2, ZB_ALL_AT + 2 * KIB)
        zi_b = interleave(1, CHUNK_B)
        pair_sums(1, CHUNK_C, 0, ZB_ALL_AT + 3 * KIB)
        z_a = quantize_z(1, CHUNK_A, zi_a)
        pair_sums(1, CHUNK_C, 2, ZB_A_AT)
        zi_c = interleave(1, CHUNK_C)
        z_b = quantize_z(1, CHUNK_B, zi_b)
        last_stage(CHUNK_A, z_all, z_a)
        z_c = quantize_z(1, CHUNK_C, zi_c)
        last_stage(CHUNK_B, z_all, z_b)
        last_stage(CHUNK_C, z_all, z_c)
